import numpy as np
import ml_dtypes


def mxq(x, axis, fmt="e4m3"):
    dtype, down = {"e4m3": (ml_dtypes.float8_e4m3fn, 7), "e5m2": (ml_dtypes.float8_e5m2, 14)}[fmt]
    v = np.moveaxis(np.asarray(x, np.float32).astype(ml_dtypes.bfloat16).astype(np.float64), axis, -1)
    blocks = v.reshape(v.shape[:-1] + (-1, 32))
    amax = np.abs(blocks).max(-1, keepdims=True)
    byte = np.maximum(np.where(amax > 0, np.frexp(amax)[1] - 1 + 127, 0) - down, 1)
    scale = np.exp2(byte - 127.0)
    codes = (blocks / scale).astype(np.float32).astype(dtype).astype(np.float64)
    return np.moveaxis((codes * scale).reshape(v.shape), -1, axis)


WIDE = False


def mx_kscale(k):
    if not WIDE:
        return np.ones(k)
    levels = np.array([10, -10, 5, -5, 0])
    if k % 512:
        return np.exp2(np.random.permutation(np.resize(levels, k // 32))).repeat(32)
    a = np.empty((k // 512, 16))
    for p in range(k // 512):
        a[p, :8] = np.random.permutation(np.resize(levels, 8))
        for g in range(8):
            far = levels[np.abs(levels - a[p, g]) >= 10]
            a[p, g + 8] = far[np.random.randint(len(far))]
    return np.exp2(a.ravel()).repeat(32)


BF16 = ml_dtypes.bfloat16


def bf(x):
    return np.asarray(x, np.float32).astype(BF16)


def f64(x):
    return np.asarray(x).astype(np.float64)


E2M1 = np.array([0.0, 0.5, 1.0, 1.5, 2.0, 3.0, 4.0, 6.0, -0.0, -0.5, -1.0, -1.5, -2.0, -3.0, -4.0, -6.0])


def pack_weight(w, fmt):
    k, n = w.shape
    w = f64(bf(w)).reshape(k // 32, 32, n)
    amax = np.abs(w).max(1)
    if fmt == "e4m3":
        byte = np.frexp(amax)[1] - 1 + 127 - 7
    else:
        mant, ex = np.frexp(amax / 6.0)
        byte = np.where(mant > 0.5, ex, ex - 1) + 127
    byte = np.clip(np.where(amax > 0, byte, 1), 1, 254)
    scaled = (w * np.exp2(127.0 - byte)[:, None, :]).reshape(k, n).astype(np.float32)
    by_word = np.ascontiguousarray(scaled.reshape(k // 512, 128, 4, n).transpose(0, 1, 3, 2))
    if fmt == "e4m3":
        words = by_word.astype(ml_dtypes.float8_e4m3fn).view(np.uint8)
    else:
        c = by_word.astype(ml_dtypes.float4_e2m1fn).view(np.uint8) & 0xF
        words = c[..., 0::2] | (c[..., 1::2] << 4)
    return np.ascontiguousarray(words), np.ascontiguousarray(byte.astype(np.uint8).reshape(k // 512, 16, n))


def unpack_weight(words, scales, fmt):
    g, p, n, _ = words.shape
    if fmt == "e4m3":
        vals = np.ascontiguousarray(words).view(ml_dtypes.float8_e4m3fn).astype(np.float64)
    else:
        nib = np.empty((g, p, n, 4), np.uint8)
        nib[..., 0::2] = words & 0xF
        nib[..., 1::2] = words >> 4
        vals = E2M1[nib]
    vals = vals * np.repeat(np.exp2(scales.astype(np.float64) - 127.0), 8, axis=1)[..., None]
    return vals.transpose(0, 1, 3, 2).reshape(g * 512, n)


B, DI, D = 1024, 512, 512


def sigmoid(v):
    return 1.0 / (1.0 + np.exp(-v))


def draw0():
    p, q = mx_kscale(DI), mx_kscale(D)
    x = bf(np.random.standard_normal((B, DI)) * p)
    h = bf(np.random.standard_normal((B, D)) * 0.5)
    t = bf(np.random.standard_normal((B, D)))
    wx_words, wx_scales = pack_weight(np.random.standard_normal((DI, 4 * D)) / np.sqrt(DI) / p[:, None], "e4m3")
    uh = bf(np.random.standard_normal((D, 2 * D)) * 2.0 / np.sqrt(D))
    g = bf((1.0 + 0.1 * np.random.standard_normal(D)) * q)
    un_words, un_scales = pack_weight(np.random.standard_normal((D, D)) * 3.0 / np.sqrt(D) / q[:, None], "e4m3")
    return {
        "x": x,
        "h": h,
        "t": t,
        "wx_words": wx_words,
        "wx_scales": wx_scales,
        "uh": uh,
        "g": g,
        "un_words": un_words,
        "un_scales": un_scales,
    }


def core(x, h, t, wx_words, wx_scales, uh, g, un_words, un_scales):
    d = h.shape[-1]
    hf = f64(h)

    gx = mxq(f64(x), 1, "e4m3") @ unpack_weight(wx_words, wx_scales, "e4m3")
    xa = gx[:, :d]
    xu = gx[:, d:2 * d]
    xr = gx[:, 2 * d:3 * d]
    xn = gx[:, 3 * d:]

    gh = f64(h) @ f64(uh)
    hu = gh[:, :d]
    hr = gh[:, d:]

    a = sigmoid(np.sum(xa * f64(t), axis=-1) / np.sqrt(d))

    u = sigmoid(xu + hu)
    r = sigmoid(xr + hr)

    s = r * hf * f64(g)[None, :]

    n = np.tanh(xn + (mxq(s, 1, "e4m3") @ unpack_weight(un_words, un_scales, "e4m3")))

    ua = a[:, None] * u

    return (1.0 - ua) * hf + ua * n


def e4m3fn_bytes(y):
    return np.clip(np.asarray(y, np.float64), -448.0, 448.0).astype(np.float32).astype(ml_dtypes.float8_e4m3fn).view(np.uint8)


def e4m3fn_values(b):
    return np.asarray(b, np.uint8).view(ml_dtypes.float8_e4m3fn).astype(np.float64)


def setup_inputs():
    d = draw0()
    x0 = np.asarray(d['x']).astype(np.float64)
    s = (np.max(np.abs(x0), axis=(0,), keepdims=True) / 448.0).astype(np.float32)
    out = {}
    for k, v in d.items():
        if k == 'x':
            out['x_bytes'] = e4m3fn_bytes(x0 / s.astype(np.float64))
            out['x_scale'] = s
        else:
            out[k] = v
    return out


def reference(x_bytes, x_scale, h, t, wx_words, wx_scales, uh, g, un_words, un_scales):
    return core(e4m3fn_values(x_bytes) * x_scale.astype(np.float64), h, t, wx_words, wx_scales, uh, g, un_words, un_scales)

@@ -1,0 +1,360 @@
+import math
+from contextlib import ExitStack
+
+import concourse.mybir as mybir
+from concourse.masks import make_identity
+
+B, D = 1024, 512
+FLOPS = 2 * B * D * (4 * D + 2 * D + D)
+
+F32 = mybir.dt.float32
+BF16 = mybir.dt.bfloat16
+I32 = mybir.dt.int32
+U32 = mybir.dt.uint32
+U8 = mybir.dt.uint8
+FP8 = mybir.dt.float8_e4m3fn
+FP8X4 = mybir.dt.float8_e4m3fn_x4
+ACT = mybir.ActivationFunctionType
+ALU = mybir.AluOpType
+
+P = 128
+TILES = B // P
+GATE_A, GATE_U, GATE_R, GATE_N = 0, 1, 2, 3
+
+
+def tile_dienaugrustep_w8_kernel(
+    tc, x_bytes, x_scale, h, t, wx_words, wx_scales, uh, g, un_words, un_scales, out
+):
+    nc = tc.nc
+    with ExitStack() as ctx:
+        keep = ctx.enter_context(tc.tile_pool(name="keep", bufs=1))
+        work = ctx.enter_context(tc.tile_pool(name="work", bufs=4))
+        psum = ctx.enter_context(tc.psum_pool(name="psum", bufs=8))
+        ctx.enter_context(tc.manual_schedule())
+
+        def bank():
+            return psum.tile([P, D], F32, name="bank", tag="bank")
+
+        ident = keep.tile([P, P], F32, name="ident")
+        make_identity(nc, ident[:])
+
+        wx_sc = keep.tile([P, D], U8, name="wx_sc", align_bytes=64)
+        un_sc = keep.tile([P, D], U8, name="un_sc", align_bytes=64)
+        nc.vector.memset(wx_sc[:].bitcast(I32), 0)
+        nc.vector.memset(un_sc[:].bitcast(I32), 0)
+
+        x_rows = x_bytes.rearrange("(p i) k -> p i k", i=TILES)
+        h_rows = h.rearrange("(p i) k -> p i k", i=TILES)
+        t_rows = t.rearrange("(p i) k -> p i k", i=TILES)
+        out_rows = out.rearrange("(p i) k -> p i k", i=TILES)
+        wx_flat = wx_words[0].rearrange("p n t -> p (n t)")
+        uh_rows = uh.rearrange("(u p e) n -> u p e n", u=2, e=2)
+
+        def load_rows(name, rows, first, count, dtype):
+            dst = keep.tile([P, count, D], dtype, name=name, align_bytes=64)
+            nc.sync.dma_start(out=dst[:], in_=rows[:, first : first + count, :])
+            return {first + i: dst[:, i, :] for i in range(count)}
+
+        def load_wx(name, first, count):
+            dst = keep.tile([P, count * D], U32, name=name, align_bytes=64)
+            nc.sync.dma_start(
+                out=dst[:].bitcast(I32),
+                in_=wx_flat[:, 4 * D * first : 4 * D * (first + count)].bitcast(I32),
+            )
+            return {first + i: dst[:, i * D : (i + 1) * D] for i in range(count)}
+
+        def load_uh(name, half, u):
+            dst = keep.tile([P, 2, D], BF16, name=name, align_bytes=64)
+            nc.sync.dma_start(out=dst[:], in_=uh_rows[u][:, :, half * D : (half + 1) * D])
+            return {(half, u, e): dst[:, e, :] for e in range(2)}
+
+        xs4 = keep.tile([P, 4], F32, name="xs4")
+        nc.sync.dma_start(out=xs4[:], in_=x_scale.rearrange("o (p t) -> p (o t)", t=4))
+        for q in range(4):
+            nc.sync.dma_start(
+                out=wx_sc[32 * q : 32 * q + 16, :].bitcast(I32),
+                in_=wx_scales[0][4 * q : 4 * q + 4, :].bitcast(I32).rearrange("r (j n) -> j r n", j=4),
+            )
+        xb = load_rows("xbytes_a", x_rows, 0, 2, U8)
+        wx = load_wx("wx_ur", GATE_U, 2)
+        hs = load_rows("h_a", h_rows, 0, 2, BF16)
+        wx = {**wx, **load_wx("wx_a", GATE_A, 1)}
+        uw = load_uh("uh_r0", 1, 0)
+        uw = {**uw, **load_uh("uh_r1", 1, 1)}
+        g4 = keep.tile([P, 2, 2], BF16, name="g4")
+        nc.sync.dma_start(out=g4[:], in_=g.rearrange("(u p e) -> p u e", u=2, e=2))
+        ts = load_rows("t_a", t_rows, 0, 2, BF16)
+        uw = {**uw, **load_uh("uh_u0", 0, 0)}
+        uw = {**uw, **load_uh("uh_u1", 0, 1)}
+        xb = {**xb, **load_rows("xbytes_b", x_rows, 2, 6, U8)}
+        wx = {**wx, **load_wx("wx_n", GATE_N, 1)}
+        un = keep.tile([P, D], U32, name="un", align_bytes=64)
+        nc.sync.dma_start(
+            out=un[:].bitcast(I32), in_=un_words[0].rearrange("p n t -> p (n t)").bitcast(I32)
+        )
+        for q in range(4):
+            nc.sync.dma_start(
+                out=un_sc[32 * q : 32 * q + 4, :].bitcast(I32),
+                in_=un_scales[0][4 * q : 4 * q + 4, :].bitcast(I32),
+            )
+        for first in range(2, TILES, 2):
+            hs = {**hs, **load_rows("h_%d" % first, h_rows, first, 2, BF16)}
+            ts = {**ts, **load_rows("t_%d" % first, t_rows, first, 2, BF16)}
+
+        def wx_scale(gate):
+            return wx_sc[4 * gate : P, :]
+
+        spread = bank()
+        for k in range(4):
+            nc.tensor.transpose(
+                spread[:, k * P : (k + 1) * P], xs4[:, k : k + 1].to_broadcast([P, P]), ident[:]
+            )
+        xs_all = keep.tile([P, D], F32, name="xs_all")
+        nc.vector.tensor_copy(
+            out=xs_all[:].rearrange("q (p t) -> q p t", t=4),
+            in_=spread[:].rearrange("q (t p) -> q p t", t=4),
+        )
+        g_diag = keep.tile([P, 4, P], BF16, name="g_diag")
+
+        st = {}
+
+        def widen_x(j):
+            xw = work.tile([P, D], BF16, name="xw", align_bytes=64)
+            nc.vector.tensor_tensor(out=xw[:], in0=xb[j].bitcast(FP8), in1=xs_all[:], op=ALU.mult)
+            st["xw", j] = xw
+
+        def turn(key, j, words):
+            b = bank()
+            for u in range(2):
+                nc.tensor.transpose(b[:, u * P : (u + 1) * P], words(u), ident[:])
+            st[key, j] = b
+
+        def turn_x(j):
+            w = st["xw", j][:].bitcast(F32)
+            turn("xT", j, lambda u: w[:, u : 2 * P : 2])
+
+        def turn_h(j):
+            w = hs[j].bitcast(F32)
+            turn("hT", j, lambda u: w[:, u * P : (u + 1) * P])
+
+        def turn_s(j):
+            w = st["s", j][:].bitcast(F32)
+            turn("sT", j, lambda u: w[:, u * P : (u + 1) * P])
+
+        def gather_words(key, j):
+            grouped = work.tile([P, D], BF16, name=key + "_grouped", align_bytes=64)
+            nc.scalar.copy(
+                out=grouped[:].bitcast(F32).rearrange("p (r u) -> p r u", u=2),
+                in_=st[key + "T", j][:, 0 : 2 * P].rearrange("p (u r) -> p r u", u=2),
+            )
+            st[key + "g", j] = grouped
+
+        def quantize(key, j):
+            codes = work.tile([P, P], U32, name=key + "_codes", align_bytes=64)
+            scales = work.tile([P, P], U8, name=key + "_scales", align_bytes=64)
+            nc.vector.quantize_mx(out=codes[:].bitcast(FP8X4), scales=scales[:], in_=st[key + "g", j][:])
+            st[key + "q", j] = (codes, scales)
+
+        def copy_hT(j):
+            hT = work.tile([P, 2 * P], F32, name="hT_words")
+            nc.scalar.copy(out=hT[:], in_=st["hT", j][:, 0 : 2 * P])
+            st["hTs", j] = hT
+
+        def h_plane(j, u, e):
+            return st["hTs", j][:].bitcast(BF16)[:, u * 2 * P + e : (u + 1) * 2 * P : 2]
+
+        def x_proj_turned(gate, j):
+            codes, scales = st["xq", j]
+            b = bank()
+            for c in range(4):
+                cols = slice(c * P, (c + 1) * P)
+                nc.tensor.matmul_mx(
+                    out=b[:, cols],
+                    lhsT=wx[gate][:, cols].bitcast(FP8X4),
+                    lhsT_scale=wx_scale(gate)[:, cols],
+                    rhs=codes[:].bitcast(FP8X4),
+                    rhs_scale=scales[:],
+                    start=True,
+                    stop=True,
+                )
+            st["xp", gate, j] = b
+
+        def copy_proj(gate, j):
+            sb = work.tile([P, D], F32, name="xp_%d" % gate)
+            nc.scalar.copy(out=sb[:], in_=st["xp", gate, j][:])
+            st["xps", gate, j] = sb
+
+        def mx_pass(b, operand, words, scale, start, stop):
+            codes, scales = operand
+            nc.tensor.matmul_mx(
+                out=b[:],
+                lhsT=codes[:].bitcast(FP8X4),
+                lhsT_scale=scales[:],
+                rhs=words.bitcast(FP8X4),
+                rhs_scale=scale,
+                start=start,
+                stop=stop,
+            )
+
+        def attention_proj(j):
+            b = bank()
+            mx_pass(b, st["xq", j], wx[GATE_A], wx_scale(GATE_A), True, True)
+            st["xa", j] = b
+
+        def candidate_proj(j):
+            b = bank()
+            mx_pass(b, st["xq", j], wx[GATE_N], wx_scale(GATE_N), True, False)
+            mx_pass(b, st["sq", j], un[:], un_sc[:], False, True)
+            st["zn", j] = b
+
+        def state_pass(gate, j, k):
+            if k == 0:
+                st["z", gate, j] = bank()
+            half = 0 if gate == GATE_U else 1
+            nc.tensor.matmul(
+                st["z", gate, j][:],
+                lhsT=h_plane(j, k // 2, k % 2),
+                rhs=uw[half, k // 2, k % 2],
+                start=(k == 0),
+                stop=(k == 3),
+            )
+
+        def add_turned(gate, j, blocks):
+            for c in blocks:
+                cols = slice(c * P, (c + 1) * P)
+                nc.tensor.matmul(
+                    st["z", gate, j][:, cols],
+                    lhsT=st["xps", gate, j][:, cols],
+                    rhs=ident[:],
+                    start=False,
+                    stop=False,
+                    is_transpose=True,
+                )
+
+        def gained_state(j):
+            b = bank()
+            for u in range(2):
+                for e in range(2):
+                    c = 2 * e + u
+                    nc.tensor.matmul(
+                        b[:, c * P : (c + 1) * P],
+                        lhsT=h_plane(j, u, e),
+                        rhs=g_diag[:, 2 * u + e, :],
+                        start=True,
+                        stop=True,
+                    )
+            st["hg", j] = b
+
+        def attention_dot(j):
+            prod = work.tile([P, D], F32, name="prod")
+            dot = work.tile([P, 1], F32, name="dot")
+            nc.vector.scalar_tensor_tensor(
+                out=prod[:], in0=st["xa", j][:], scalar=1.0 / math.sqrt(D), in1=ts[j],
+                op0=ALU.mult, op1=ALU.mult, accum_out=dot[:],
+            )
+            st["dot", j] = dot
+
+        def attention_gate(j):
+            a = work.tile([P, 1], F32, name="a")
+            nc.scalar.activation(out=a[:], in_=st["dot", j][:], func=ACT.Sigmoid)
+            st["a", j] = a
+
+        def reset_gate(j):
+            r = work.tile([P, D], F32, name="r")
+            nc.scalar.activation(
+                out=r[:].rearrange("q (u p e) -> q u p e", u=2, e=2),
+                in_=st["z", GATE_R, j][:].rearrange("q (p u e) -> q u p e", u=2, e=2),
+                func=ACT.Sigmoid,
+            )
+            st["r", j] = r
+
+        def update_gate(j):
+            ug = work.tile([P, D], F32, name="ug")
+            nc.scalar.activation(out=ug[:], in_=st["z", GATE_U, j][:], func=ACT.Sigmoid)
+            st["u", j] = ug
+
+        def reset_state(j):
+            s = work.tile([P, D], BF16, name="s", align_bytes=64)
+            nc.vector.tensor_tensor(
+                out=s[:].rearrange("q (u p e) -> q u p e", u=2, e=2),
+                in0=st["hg", j][:].rearrange("q (e p u) -> q u p e", u=2, e=2),
+                in1=st["r", j][:].rearrange("q (u p e) -> q u p e", u=2, e=2),
+                op=ALU.mult,
+            )
+            st["s", j] = s
+
+        def candidate(j):
+            n = work.tile([P, D], F32, name="n")
+            nc.scalar.activation(out=n[:], in_=st["zn", j][:], func=ACT.Tanh)
+            st["n", j] = n
+
+        def step_delta(j):
+            d = work.tile([P, D], F32, name="d")
+            nc.vector.tensor_tensor(out=d[:], in0=st["n", j][:], in1=hs[j], op=ALU.subtract)
+            st["d", j] = d
+
+        def step_scale(j):
+            m = work.tile([P, D], F32, name="m")
+            nc.vector.scalar_tensor_tensor(
+                out=m[:], in0=st["u", j][:], scalar=st["a", j][:], in1=st["d", j][:],
+                op0=ALU.mult, op1=ALU.mult,
+            )
+            st["m", j] = m
+
+        def step_finish(j):
+            o = work.tile([P, D], F32, name="o")
+            nc.vector.tensor_tensor(out=o[:], in0=st["m", j][:], in1=hs[j], op=ALU.add)
+            nc.sync.dma_start(out=out_rows[:, j, :], in_=o[:])
+
+        def make_g_diag():
+            nc.vector.tensor_tensor(
+                out=g_diag[:],
+                in0=ident[:].unsqueeze(1).to_broadcast([P, 4, P]),
+                in1=g4[:].rearrange("p u e -> p (u e)").unsqueeze(2).to_broadcast([P, 4, P]),
+                op=ALU.mult,
+            )
+
+        def on(fn, j, *args):
+            if 0 <= j < TILES:
+                fn(*args[:1], j, *args[1:]) if args else fn(j)
+
+        for j in range(-1, TILES + 2):
+            on(update_gate, j - 1)
+            on(step_scale, j - 2)
+            on(x_proj_turned, j, GATE_R)
+            on(copy_proj, j, GATE_R)
+            on(x_proj_turned, j, GATE_U)
+            on(attention_proj, j)
+            on(widen_x, j + 1)
+            on(step_finish, j - 2)
+            on(state_pass, j, GATE_R, 0)
+            on(turn_s, j - 1)
+            on(gather_words, j - 1, "s")
+            on(copy_proj, j, GATE_U)
+            on(attention_dot, j)
+            on(state_pass, j, GATE_R, 1)
+            on(add_turned, j, GATE_R, (0, 1))
+            on(state_pass, j, GATE_R, 2)
+            on(add_turned, j, GATE_R, (2, 3))
+            on(state_pass, j, GATE_R, 3)
+            on(quantize, j - 1, "s")
+            if j == 0:
+                make_g_diag()
+            on(attention_gate, j)
+            on(reset_gate, j)
+            on(turn_x, j + 1)
+            on(gather_words, j + 1, "x")
+            on(gained_state, j)
+            on(reset_state, j)
+            on(quantize, j + 1, "x")
+            on(candidate_proj, j - 1)
+            on(candidate, j - 1)
+            on(state_pass, j, GATE_U, 0)
+            on(turn_h, j + 1)
+            on(copy_hT, j + 1)
+            on(state_pass, j, GATE_U, 1)
+            on(add_turned, j, GATE_U, (0, 1))
+            on(state_pass, j, GATE_U, 2)
+            on(add_turned, j, GATE_U, (2, 3))
+            on(state_pass, j, GATE_U, 3)
+            on(step_delta, j - 1)

@@ -68,25 +68,31 @@ def tile_dienaugrustep_w8_kernel(
             nc.sync.dma_start(out=dst[:], in_=uh_rows[u][:, :, half * D : (half + 1) * D])
             return {(half, u, e): dst[:, e, :] for e in range(2)}
 
+        warm = keep.tile([P, 1], F32, name="warm")
+        nc.scalar.activation(out=warm[:], in_=ident[:, 0:1], func=ACT.Sigmoid)
+
         xs4 = keep.tile([P, 4], F32, name="xs4")
         nc.sync.dma_start(out=xs4[:], in_=x_scale.rearrange("o (p t) -> p (o t)", t=4))
+        xb = load_rows("xbytes_a", x_rows, 0, 2, U8)
+        hs = load_rows("h_0", h_rows, 0, 2, BF16)
+        uw = load_uh("uh_r0", 1, 0)
         for q in range(4):
             nc.sync.dma_start(
                 out=wx_sc[32 * q : 32 * q + 16, :].bitcast(I32),
                 in_=wx_scales[0][4 * q : 4 * q + 4, :].bitcast(I32).rearrange("r (j n) -> j r n", j=4),
             )
-        xb = load_rows("xbytes_a", x_rows, 0, 2, U8)
-        wx = load_wx("wx_ur", GATE_U, 2)
-        hs = load_rows("h_a", h_rows, 0, 2, BF16)
-        wx = {**wx, **load_wx("wx_a", GATE_A, 1)}
-        uw = load_uh("uh_r0", 1, 0)
         uw = {**uw, **load_uh("uh_r1", 1, 1)}
-        g4 = keep.tile([P, 2, 2], BF16, name="g4")
-        nc.sync.dma_start(out=g4[:], in_=g.rearrange("(u p e) -> p u e", u=2, e=2))
-        ts = load_rows("t_a", t_rows, 0, 2, BF16)
+        xb = {**xb, **load_rows("xbytes_b", x_rows, 2, 2, U8)}
+        wx = load_wx("wx_r", GATE_R, 1)
         uw = {**uw, **load_uh("uh_u0", 0, 0)}
         uw = {**uw, **load_uh("uh_u1", 0, 1)}
-        xb = {**xb, **load_rows("xbytes_b", x_rows, 2, 6, U8)}
+        g4 = keep.tile([P, 2, 2], BF16, name="g4")
+        nc.sync.dma_start(out=g4[:], in_=g.rearrange("(u p e) -> p u e", u=2, e=2))
+        hs = {**hs, **load_rows("h_2", h_rows, 2, 2, BF16)}
+        xb = {**xb, **load_rows("xbytes_c", x_rows, 4, 4, U8)}
+        wx = {**wx, **load_wx("wx_u", GATE_U, 1)}
+        wx = {**wx, **load_wx("wx_a", GATE_A, 1)}
+        ts = load_rows("t_0", t_rows, 0, 2, BF16)
         wx = {**wx, **load_wx("wx_n", GATE_N, 1)}
         un = keep.tile([P, D], U32, name="un", align_bytes=64)
         nc.sync.dma_start(
@@ -97,9 +103,11 @@ def tile_dienaugrustep_w8_kernel(
                 out=un_sc[32 * q : 32 * q + 4, :].bitcast(I32),
                 in_=un_scales[0][4 * q : 4 * q + 4, :].bitcast(I32),
             )
-        for first in range(2, TILES, 2):
-            hs = {**hs, **load_rows("h_%d" % first, h_rows, first, 2, BF16)}
-            ts = {**ts, **load_rows("t_%d" % first, t_rows, first, 2, BF16)}
+        hs = {**hs, **load_rows("h_4", h_rows, 4, 2, BF16)}
+        ts = {**ts, **load_rows("t_2", t_rows, 2, 2, BF16)}
+        hs = {**hs, **load_rows("h_6", h_rows, 6, 2, BF16)}
+        ts = {**ts, **load_rows("t_4", t_rows, 4, 2, BF16)}
+        ts = {**ts, **load_rows("t_6", t_rows, 6, 2, BF16)}
 
         def wx_scale(gate):
             return wx_sc[4 * gate : P, :]
@@ -163,27 +171,6 @@ def tile_dienaugrustep_w8_kernel(
         def h_plane(j, u, e):
             return st["hTs", j][:].bitcast(BF16)[:, u * 2 * P + e : (u + 1) * 2 * P : 2]
 
-        def x_proj_turned(gate, j):
-            codes, scales = st["xq", j]
-            b = bank()
-            for c in range(4):
-                cols = slice(c * P, (c + 1) * P)
-                nc.tensor.matmul_mx(
-                    out=b[:, cols],
-                    lhsT=wx[gate][:, cols].bitcast(FP8X4),
-                    lhsT_scale=wx_scale(gate)[:, cols],
-                    rhs=codes[:].bitcast(FP8X4),
-                    rhs_scale=scales[:],
-                    start=True,
-                    stop=True,
-                )
-            st["xp", gate, j] = b
-
-        def copy_proj(gate, j):
-            sb = work.tile([P, D], F32, name="xp_%d" % gate)
-            nc.scalar.copy(out=sb[:], in_=st["xp", gate, j][:])
-            st["xps", gate, j] = sb
-
         def mx_pass(b, operand, words, scale, start, stop):
             codes, scales = operand
             nc.tensor.matmul_mx(
@@ -196,10 +183,10 @@ def tile_dienaugrustep_w8_kernel(
                 stop=stop,
             )
 
-        def attention_proj(j):
+        def x_proj(gate, j):
             b = bank()
-            mx_pass(b, st["xq", j], wx[GATE_A], wx_scale(GATE_A), True, True)
-            st["xa", j] = b
+            mx_pass(b, st["xq", j], wx[gate], wx_scale(gate), True, True)
+            st["xp", gate, j] = b
 
         def candidate_proj(j):
             b = bank()
@@ -219,17 +206,35 @@ def tile_dienaugrustep_w8_kernel(
                 stop=(k == 3),
             )
 
-        def add_turned(gate, j, blocks):
-            for c in blocks:
-                cols = slice(c * P, (c + 1) * P)
-                nc.tensor.matmul(
-                    st["z", gate, j][:, cols],
-                    lhsT=st["xps", gate, j][:, cols],
-                    rhs=ident[:],
-                    start=False,
-                    stop=False,
-                    is_transpose=True,
-                )
+        def in_gate_order(gate, src):
+            if gate == GATE_R:
+                return src.rearrange("q (p u e) -> q u p e", u=2, e=2)
+            return src
+
+        def as_gate_shape(gate, dst):
+            if gate == GATE_R:
+                return dst.rearrange("q (u p e) -> q u p e", u=2, e=2)
+            return dst
+
+        def copy_state_proj(gate, j):
+            sb = work.tile([P, D], F32, name="hp_%d" % gate)
+            nc.scalar.copy(out=as_gate_shape(gate, sb[:]), in_=in_gate_order(gate, st["z", gate, j][:]))
+            st["hp", gate, j] = sb
+
+        def add_proj(gate, j):
+            z = work.tile([P, D], F32, name="z_%d" % gate)
+            nc.vector.tensor_tensor(
+                out=as_gate_shape(gate, z[:]),
+                in0=in_gate_order(gate, st["xp", gate, j][:]),
+                in1=as_gate_shape(gate, st["hp", gate, j][:]),
+                op=ALU.add,
+            )
+            st["zs", gate, j] = z
+
+        def gate_sigmoid(gate, j):
+            y = work.tile([P, D], F32, name="gate_%d" % gate)
+            nc.scalar.activation(out=y[:], in_=st["zs", gate, j][:], func=ACT.Sigmoid)
+            st["gate", gate, j] = y
 
         def gained_state(j):
             b = bank()
@@ -249,7 +254,7 @@ def tile_dienaugrustep_w8_kernel(
             prod = work.tile([P, D], F32, name="prod")
             dot = work.tile([P, 1], F32, name="dot")
             nc.vector.scalar_tensor_tensor(
-                out=prod[:], in0=st["xa", j][:], scalar=1.0 / math.sqrt(D), in1=ts[j],
+                out=prod[:], in0=st["xp", GATE_A, j][:], scalar=1.0 / math.sqrt(D), in1=ts[j],
                 op0=ALU.mult, op1=ALU.mult, accum_out=dot[:],
             )
             st["dot", j] = dot
@@ -259,26 +264,12 @@ def tile_dienaugrustep_w8_kernel(
             nc.scalar.activation(out=a[:], in_=st["dot", j][:], func=ACT.Sigmoid)
             st["a", j] = a
 
-        def reset_gate(j):
-            r = work.tile([P, D], F32, name="r")
-            nc.scalar.activation(
-                out=r[:].rearrange("q (u p e) -> q u p e", u=2, e=2),
-                in_=st["z", GATE_R, j][:].rearrange("q (p u e) -> q u p e", u=2, e=2),
-                func=ACT.Sigmoid,
-            )
-            st["r", j] = r
-
-        def update_gate(j):
-            ug = work.tile([P, D], F32, name="ug")
-            nc.scalar.activation(out=ug[:], in_=st["z", GATE_U, j][:], func=ACT.Sigmoid)
-            st["u", j] = ug
-
         def reset_state(j):
             s = work.tile([P, D], BF16, name="s", align_bytes=64)
             nc.vector.tensor_tensor(
                 out=s[:].rearrange("q (u p e) -> q u p e", u=2, e=2),
                 in0=st["hg", j][:].rearrange("q (e p u) -> q u p e", u=2, e=2),
-                in1=st["r", j][:].rearrange("q (u p e) -> q u p e", u=2, e=2),
+                in1=st["gate", GATE_R, j][:].rearrange("q (u p e) -> q u p e", u=2, e=2),
                 op=ALU.mult,
             )
             st["s", j] = s
@@ -296,7 +287,7 @@ def tile_dienaugrustep_w8_kernel(
         def step_scale(j):
             m = work.tile([P, D], F32, name="m")
             nc.vector.scalar_tensor_tensor(
-                out=m[:], in0=st["u", j][:], scalar=st["a", j][:], in1=st["d", j][:],
+                out=m[:], in0=st["gate", GATE_U, j][:], scalar=st["a", j][:], in1=st["d", j][:],
                 op0=ALU.mult, op1=ALU.mult,
             )
             st["m", j] = m
@@ -318,43 +309,65 @@ def tile_dienaugrustep_w8_kernel(
             if 0 <= j < TILES:
                 fn(*args[:1], j, *args[1:]) if args else fn(j)
 
-        for j in range(-1, TILES + 2):
-            on(update_gate, j - 1)
-            on(step_scale, j - 2)
-            on(x_proj_turned, j, GATE_R)
-            on(copy_proj, j, GATE_R)
-            on(x_proj_turned, j, GATE_U)
-            on(attention_proj, j)
-            on(widen_x, j + 1)
-            on(step_finish, j - 2)
-            on(state_pass, j, GATE_R, 0)
+        for j in range(-3, TILES):
+            on(step_scale, j - 3)
+            on(x_proj, j - 1, GATE_U)
+            on(x_proj, j, GATE_R)
+            on(reset_state, j - 1)
+            on(add_proj, j - 1, GATE_U)
+            on(candidate_proj, j - 2)
+            on(candidate, j - 2)
+            on(add_proj, j, GATE_R)
+            on(gate_sigmoid, j - 1, GATE_U)
+            on(x_proj, j - 1, GATE_A)
+            on(gate_sigmoid, j, GATE_R)
+            on(state_pass, j, GATE_U, 0)
             on(turn_s, j - 1)
+            on(state_pass, j, GATE_U, 1)
+            on(turn_x, j + 1)
+            on(widen_x, j + 3)
+            on(attention_dot, j - 1)
+            on(step_finish, j - 3)
             on(gather_words, j - 1, "s")
-            on(copy_proj, j, GATE_U)
-            on(attention_dot, j)
-            on(state_pass, j, GATE_R, 1)
-            on(add_turned, j, GATE_R, (0, 1))
-            on(state_pass, j, GATE_R, 2)
-            on(add_turned, j, GATE_R, (2, 3))
-            on(state_pass, j, GATE_R, 3)
+            on(gather_words, j + 1, "x")
+            on(state_pass, j, GATE_U, 2)
+            on(state_pass, j, GATE_U, 3)
+            on(attention_gate, j - 1)
+            on(copy_state_proj, j, GATE_U)
+            on(step_delta, j - 2)
             on(quantize, j - 1, "s")
+            on(quantize, j + 1, "x")
             if j == 0:
                 make_g_diag()
-            on(attention_gate, j)
-            on(reset_gate, j)
-            on(turn_x, j + 1)
-            on(gather_words, j + 1, "x")
             on(gained_state, j)
-            on(reset_state, j)
-            on(quantize, j + 1, "x")
-            on(candidate_proj, j - 1)
-            on(candidate, j - 1)
-            on(state_pass, j, GATE_U, 0)
-            on(turn_h, j + 1)
-            on(copy_hT, j + 1)
-            on(state_pass, j, GATE_U, 1)
-            on(add_turned, j, GATE_U, (0, 1))
-            on(state_pass, j, GATE_U, 2)
-            on(add_turned, j, GATE_U, (2, 3))
-            on(state_pass, j, GATE_U, 3)
-            on(step_delta, j - 1)
+            on(state_pass, j + 1, GATE_R, 0)
+            on(turn_h, j + 2)
+            on(copy_hT, j + 2)
+            on(state_pass, j + 1, GATE_R, 1)
+            on(state_pass, j + 1, GATE_R, 2)
+            on(state_pass, j + 1, GATE_R, 3)
+            on(copy_state_proj, j + 1, GATE_R)
+
+        last = TILES - 1
+        on(x_proj, last, GATE_U)
+        on(x_proj, last, GATE_A)
+        on(reset_state, last)
+        on(turn_s, last)
+        on(gather_words, last, "s")
+        on(add_proj, last, GATE_U)
+        on(gate_sigmoid, last, GATE_U)
+        on(step_scale, last - 2)
+        on(candidate_proj, last - 1)
+        on(candidate, last - 1)
+        on(quantize, last, "s")
+        on(candidate_proj, last)
+        on(attention_dot, last)
+        on(attention_gate, last)
+        on(candidate, last)
+        on(step_finish, last - 2)
+        on(step_delta, last - 1)
+        on(step_delta, last)
+        on(step_scale, last - 1)
+        on(step_scale, last)
+        on(step_finish, last - 1)
+        on(step_finish, last)

@@ -19,6 +19,7 @@ ALU = mybir.AluOpType
 
 P = 128
 TILES = B // P
+GP_TILES = 0
 GATE_A, GATE_U, GATE_R, GATE_N = 0, 1, 2, 3
 
 
@@ -50,50 +51,51 @@ def tile_dienaugrustep_w8_kernel(
         wx_flat = wx_words[0].rearrange("p n t -> p (n t)")
         uh_rows = uh.rearrange("(u p e) n -> u p e n", u=2, e=2)
 
-        def load_rows(name, rows, first, count, dtype):
+        xb, hs, ts, wx, uw = {}, {}, {}, {}, {}
+
+        def load_rows(table, name, rows, first, count, dtype):
             dst = keep.tile([P, count, D], dtype, name=name, align_bytes=64)
             nc.sync.dma_start(out=dst[:], in_=rows[:, first : first + count, :])
-            return {first + i: dst[:, i, :] for i in range(count)}
+            for i in range(count):
+                table[first + i] = dst[:, i, :]
 
         def load_wx(name, first, count):
             dst = keep.tile([P, count * D], U32, name=name, align_bytes=64)
             nc.sync.dma_start(
-                out=dst[:].bitcast(I32),
-                in_=wx_flat[:, 4 * D * first : 4 * D * (first + count)].bitcast(I32),
+                out=dst[:].bitcast(I32), in_=wx_flat[:, 4 * D * first : 4 * D * (first + count)].bitcast(I32)
             )
-            return {first + i: dst[:, i * D : (i + 1) * D] for i in range(count)}
+            for i in range(count):
+                wx[first + i] = dst[:, i * D : (i + 1) * D]
 
-        def load_uh(name, half, u):
-            dst = keep.tile([P, 2, D], BF16, name=name, align_bytes=64)
-            nc.sync.dma_start(out=dst[:], in_=uh_rows[u][:, :, half * D : (half + 1) * D])
-            return {(half, u, e): dst[:, e, :] for e in range(2)}
+        def load_uh(name, u):
+            dst = keep.tile([P, 2, 2 * D], BF16, name=name, align_bytes=64)
+            nc.sync.dma_start(out=dst[:], in_=uh_rows[u])
+            for e in range(2):
+                uw[GATE_U, u, e] = dst[:, e, 0:D]
+                uw[GATE_R, u, e] = dst[:, e, D : 2 * D]
 
         warm = keep.tile([P, 1], F32, name="warm")
         nc.scalar.activation(out=warm[:], in_=ident[:, 0:1], func=ACT.Sigmoid)
 
-        xs4 = keep.tile([P, 4], F32, name="xs4")
-        nc.sync.dma_start(out=xs4[:], in_=x_scale.rearrange("o (p t) -> p (o t)", t=4))
-        xb = load_rows("xbytes_a", x_rows, 0, 2, U8)
-        hs = load_rows("h_0", h_rows, 0, 2, BF16)
-        uw = load_uh("uh_r0", 1, 0)
         for q in range(4):
-            nc.sync.dma_start(
+            nc.gpsimd.dma_start(
                 out=wx_sc[32 * q : 32 * q + 16, :].bitcast(I32),
                 in_=wx_scales[0][4 * q : 4 * q + 4, :].bitcast(I32).rearrange("r (j n) -> j r n", j=4),
             )
-        uw = {**uw, **load_uh("uh_r1", 1, 1)}
-        xb = {**xb, **load_rows("xbytes_b", x_rows, 2, 2, U8)}
-        wx = load_wx("wx_r", GATE_R, 1)
-        uw = {**uw, **load_uh("uh_u0", 0, 0)}
-        uw = {**uw, **load_uh("uh_u1", 0, 1)}
+        xs4 = keep.tile([P, 4], F32, name="xs4")
+        nc.sync.dma_start(out=xs4[:], in_=x_scale.rearrange("o (p t) -> p (o t)", t=4))
+        load_rows(xb, "xbytes_0", x_rows, 0, 2, U8)
+        load_rows(hs, "h_0", h_rows, 0, 2, BF16)
         g4 = keep.tile([P, 2, 2], BF16, name="g4")
         nc.sync.dma_start(out=g4[:], in_=g.rearrange("(u p e) -> p u e", u=2, e=2))
-        hs = {**hs, **load_rows("h_2", h_rows, 2, 2, BF16)}
-        xb = {**xb, **load_rows("xbytes_c", x_rows, 4, 4, U8)}
-        wx = {**wx, **load_wx("wx_u", GATE_U, 1)}
-        wx = {**wx, **load_wx("wx_a", GATE_A, 1)}
-        ts = load_rows("t_0", t_rows, 0, 2, BF16)
-        wx = {**wx, **load_wx("wx_n", GATE_N, 1)}
+        load_uh("uh_0", 0)
+        load_uh("uh_1", 1)
+        load_wx("wx_ur", GATE_U, 2)
+        load_wx("wx_a", GATE_A, 1)
+        load_rows(hs, "h_2", h_rows, 2, 2, BF16)
+        load_rows(xb, "xbytes_2", x_rows, 2, 2, U8)
+        load_rows(ts, "t_0", t_rows, 0, 2, BF16)
+        load_wx("wx_n", GATE_N, 1)
         un = keep.tile([P, D], U32, name="un", align_bytes=64)
         nc.sync.dma_start(
             out=un[:].bitcast(I32), in_=un_words[0].rearrange("p n t -> p (n t)").bitcast(I32)
@@ -103,11 +105,12 @@ def tile_dienaugrustep_w8_kernel(
                 out=un_sc[32 * q : 32 * q + 4, :].bitcast(I32),
                 in_=un_scales[0][4 * q : 4 * q + 4, :].bitcast(I32),
             )
-        hs = {**hs, **load_rows("h_4", h_rows, 4, 2, BF16)}
-        ts = {**ts, **load_rows("t_2", t_rows, 2, 2, BF16)}
-        hs = {**hs, **load_rows("h_6", h_rows, 6, 2, BF16)}
-        ts = {**ts, **load_rows("t_4", t_rows, 4, 2, BF16)}
-        ts = {**ts, **load_rows("t_6", t_rows, 6, 2, BF16)}
+        load_rows(xb, "xbytes_4", x_rows, 4, 4, U8)
+        load_rows(hs, "h_4", h_rows, 4, 2, BF16)
+        load_rows(ts, "t_2", t_rows, 2, 2, BF16)
+        load_rows(hs, "h_6", h_rows, 6, 2, BF16)
+        load_rows(ts, "t_4", t_rows, 4, 2, BF16)
+        load_rows(ts, "t_6", t_rows, 6, 2, BF16)
 
         def wx_scale(gate):
             return wx_sc[4 * gate : P, :]
@@ -125,6 +128,11 @@ def tile_dienaugrustep_w8_kernel(
         g_diag = keep.tile([P, 4, P], BF16, name="g_diag")
 
         st = {}
+
+        def columns(part):
+            if part is None:
+                return slice(0, D)
+            return slice(part * D // 2, (part + 1) * D // 2)
 
         def widen_x(j):
             xw = work.tile([P, D], BF16, name="xw", align_bytes=64)
@@ -149,7 +157,7 @@ def tile_dienaugrustep_w8_kernel(
             w = st["s", j][:].bitcast(F32)
             turn("sT", j, lambda u: w[:, u * P : (u + 1) * P])
 
-        def gather_words(key, j):
+        def gather_words(j, key):
             grouped = work.tile([P, D], BF16, name=key + "_grouped", align_bytes=64)
             nc.scalar.copy(
                 out=grouped[:].bitcast(F32).rearrange("p (r u) -> p r u", u=2),
@@ -157,7 +165,7 @@ def tile_dienaugrustep_w8_kernel(
             )
             st[key + "g", j] = grouped
 
-        def quantize(key, j):
+        def quantize(j, key):
             codes = work.tile([P, P], U32, name=key + "_codes", align_bytes=64)
             scales = work.tile([P, P], U8, name=key + "_scales", align_bytes=64)
             nc.vector.quantize_mx(out=codes[:].bitcast(FP8X4), scales=scales[:], in_=st[key + "g", j][:])
@@ -183,10 +191,51 @@ def tile_dienaugrustep_w8_kernel(
                 stop=stop,
             )
 
-        def x_proj(gate, j):
+        def x_proj(j, gate):
             b = bank()
             mx_pass(b, st["xq", j], wx[gate], wx_scale(gate), True, True)
             st["xp", gate, j] = b
+
+        def x_proj_turned(j, gate):
+            codes, scales = st["xq", j]
+            b = bank()
+            for c in range(4):
+                cols = slice(c * P, (c + 1) * P)
+                nc.tensor.matmul_mx(
+                    out=b[:, cols],
+                    lhsT=wx[gate][:, cols].bitcast(FP8X4),
+                    lhsT_scale=wx_scale(gate)[:, cols],
+                    rhs=codes[:].bitcast(FP8X4),
+                    rhs_scale=scales[:],
+                    start=True,
+                    stop=True,
+                )
+            st["xp", gate, j] = b
+
+        def copy_proj(j, gate):
+            sb = work.tile([P, D], F32, name="xp_%d" % gate)
+            nc.scalar.copy(out=sb[:], in_=st["xp", gate, j][:])
+            st["xps", gate, j] = sb
+
+        def add_turned(j, gate, blocks):
+            for c in blocks:
+                cols = slice(c * P, (c + 1) * P)
+                nc.tensor.matmul(
+                    st["z", gate, j][:, cols],
+                    lhsT=st["xps", gate, j][:, cols],
+                    rhs=ident[:],
+                    start=False,
+                    stop=False,
+                    is_transpose=True,
+                )
+
+        def update_gate(j, part):
+            if part != 1:
+                st["gate", GATE_U, j] = work.tile([P, D], F32, name="gate_u")
+            cols = columns(part)
+            nc.scalar.activation(
+                out=st["gate", GATE_U, j][:, cols], in_=st["z", GATE_U, j][:, cols], func=ACT.Sigmoid
+            )
 
         def candidate_proj(j):
             b = bank()
@@ -194,14 +243,13 @@ def tile_dienaugrustep_w8_kernel(
             mx_pass(b, st["sq", j], un[:], un_sc[:], False, True)
             st["zn", j] = b
 
-        def state_pass(gate, j, k):
+        def state_pass(j, gate, k):
             if k == 0:
                 st["z", gate, j] = bank()
-            half = 0 if gate == GATE_U else 1
             nc.tensor.matmul(
                 st["z", gate, j][:],
                 lhsT=h_plane(j, k // 2, k % 2),
-                rhs=uw[half, k // 2, k % 2],
+                rhs=uw[gate, k // 2, k % 2],
                 start=(k == 0),
                 stop=(k == 3),
             )
@@ -216,12 +264,12 @@ def tile_dienaugrustep_w8_kernel(
                 return dst.rearrange("q (u p e) -> q u p e", u=2, e=2)
             return dst
 
-        def copy_state_proj(gate, j):
+        def copy_state_proj(j, gate):
             sb = work.tile([P, D], F32, name="hp_%d" % gate)
             nc.scalar.copy(out=as_gate_shape(gate, sb[:]), in_=in_gate_order(gate, st["z", gate, j][:]))
             st["hp", gate, j] = sb
 
-        def add_proj(gate, j):
+        def add_proj(j, gate):
             z = work.tile([P, D], F32, name="z_%d" % gate)
             nc.vector.tensor_tensor(
                 out=as_gate_shape(gate, z[:]),
@@ -231,7 +279,7 @@ def tile_dienaugrustep_w8_kernel(
             )
             st["zs", gate, j] = z
 
-        def gate_sigmoid(gate, j):
+        def gate_sigmoid(j, gate):
             y = work.tile([P, D], F32, name="gate_%d" % gate)
             nc.scalar.activation(out=y[:], in_=st["zs", gate, j][:], func=ACT.Sigmoid)
             st["gate", gate, j] = y
@@ -284,18 +332,23 @@ def tile_dienaugrustep_w8_kernel(
             nc.vector.tensor_tensor(out=d[:], in0=st["n", j][:], in1=hs[j], op=ALU.subtract)
             st["d", j] = d
 
-        def step_scale(j):
-            m = work.tile([P, D], F32, name="m")
-            nc.vector.scalar_tensor_tensor(
-                out=m[:], in0=st["gate", GATE_U, j][:], scalar=st["a", j][:], in1=st["d", j][:],
-                op0=ALU.mult, op1=ALU.mult,
+        def step_scale(j, part):
+            if part != 1:
+                st["m", j] = work.tile([P, D], F32, name="m")
+            cols = columns(part)
+            nc.vector.tensor_tensor(
+                out=st["m", j][:, cols], in0=st["gate", GATE_U, j][:, cols], in1=st["d", j][:, cols], op=ALU.mult
             )
-            st["m", j] = m
 
-        def step_finish(j):
-            o = work.tile([P, D], F32, name="o")
-            nc.vector.tensor_tensor(out=o[:], in0=st["m", j][:], in1=hs[j], op=ALU.add)
-            nc.sync.dma_start(out=out_rows[:, j, :], in_=o[:])
+        def step_finish(j, part):
+            if part != 1:
+                st["o", j] = work.tile([P, D], F32, name="o")
+            cols = columns(part)
+            nc.vector.scalar_tensor_tensor(
+                out=st["o", j][:, cols], in0=st["m", j][:, cols], scalar=st["a", j][:], in1=hs[j][:, cols],
+                op0=ALU.mult, op1=ALU.add,
+            )
+            nc.sync.dma_start(out=out_rows[:, j, cols], in_=st["o", j][:, cols])
 
         def make_g_diag():
             nc.vector.tensor_tensor(
@@ -307,67 +360,170 @@ def tile_dienaugrustep_w8_kernel(
 
         def on(fn, j, *args):
             if 0 <= j < TILES:
-                fn(*args[:1], j, *args[1:]) if args else fn(j)
+                fn(j, *args)
 
-        for j in range(-3, TILES):
-            on(step_scale, j - 3)
-            on(x_proj, j - 1, GATE_U)
+        on(widen_x, 0)
+        on(turn_h, 0)
+        on(copy_hT, 0)
+        on(turn_h, 1)
+        on(copy_hT, 1)
+        on(widen_x, 1)
+        make_g_diag()
+        on(state_pass, 0, GATE_R, 0)
+        on(state_pass, 0, GATE_R, 1)
+        on(turn_x, 0)
+        on(gather_words, 0, "x")
+        on(quantize, 0, "x")
+        on(state_pass, 1, GATE_R, 0)
+        on(state_pass, 1, GATE_R, 1)
+        on(state_pass, 0, GATE_R, 2)
+        on(state_pass, 0, GATE_R, 3)
+        on(copy_state_proj, 0, GATE_R)
+        on(turn_x, 1)
+        on(gather_words, 1, "x")
+        on(state_pass, 1, GATE_R, 2)
+        on(state_pass, 1, GATE_R, 3)
+        on(copy_state_proj, 1, GATE_R)
+        on(x_proj, 0, GATE_R)
+        on(add_proj, 0, GATE_R)
+        on(quantize, 1, "x")
+        on(x_proj_turned, 0, GATE_U)
+        on(copy_proj, 0, GATE_U)
+        on(gate_sigmoid, 0, GATE_R)
+        on(widen_x, 2)
+        on(widen_x, 3)
+        on(gained_state, 0)
+        on(state_pass, 0, GATE_U, 0)
+        on(turn_h, 2)
+        on(copy_hT, 2)
+        on(state_pass, 0, GATE_U, 1)
+        on(state_pass, 0, GATE_U, 2)
+        on(add_turned, 0, GATE_U, (0,))
+        on(add_turned, 0, GATE_U, (1,))
+        on(add_turned, 0, GATE_U, (2,))
+        on(add_turned, 0, GATE_U, (3,))
+        on(state_pass, 0, GATE_U, 3)
+        on(reset_state, 0)
+        on(update_gate, 0, None)
+
+        on(x_proj, 1, GATE_R)
+        on(add_proj, 1, GATE_R)
+        on(x_proj, 0, GATE_A)
+        on(state_pass, 2, GATE_R, 0)
+        on(turn_s, 0)
+        on(gather_words, 0, "s")
+        on(gate_sigmoid, 1, GATE_R)
+        on(attention_dot, 0)
+        on(quantize, 0, "s")
+        on(state_pass, 2, GATE_R, 1)
+        on(turn_x, 2)
+        on(gather_words, 2, "x")
+        on(attention_gate, 0)
+        on(state_pass, 2, GATE_R, 2)
+        on(turn_h, 3)
+        on(copy_hT, 3)
+        on(state_pass, 2, GATE_R, 3)
+        on(widen_x, 4)
+        on(quantize, 2, "x")
+        on(copy_state_proj, 2, GATE_R)
+        on(gained_state, 1)
+        on(reset_state, 1)
+        on(candidate_proj, 0)
+        on(candidate, 0)
+        on(step_delta, 0)
+
+        for j in range(2, TILES - 1):
+            on(x_proj_turned, j - 1, GATE_U)
             on(x_proj, j, GATE_R)
-            on(reset_state, j - 1)
-            on(add_proj, j - 1, GATE_U)
-            on(candidate_proj, j - 2)
-            on(candidate, j - 2)
+            on(copy_proj, j - 1, GATE_U)
             on(add_proj, j, GATE_R)
-            on(gate_sigmoid, j - 1, GATE_U)
             on(x_proj, j - 1, GATE_A)
-            on(gate_sigmoid, j, GATE_R)
-            on(state_pass, j, GATE_U, 0)
+            on(state_pass, j - 1, GATE_U, 0)
             on(turn_s, j - 1)
-            on(state_pass, j, GATE_U, 1)
-            on(turn_x, j + 1)
-            on(widen_x, j + 3)
-            on(attention_dot, j - 1)
-            on(step_finish, j - 3)
             on(gather_words, j - 1, "s")
-            on(gather_words, j + 1, "x")
-            on(state_pass, j, GATE_U, 2)
-            on(state_pass, j, GATE_U, 3)
-            on(attention_gate, j - 1)
-            on(copy_state_proj, j, GATE_U)
-            on(step_delta, j - 2)
+            on(gate_sigmoid, j, GATE_R)
+            on(step_scale, j - 2, None)
             on(quantize, j - 1, "s")
+            on(state_pass, j - 1, GATE_U, 1)
+            on(turn_x, j + 1)
+            on(gather_words, j + 1, "x")
+            on(attention_dot, j - 1)
+            on(state_pass, j - 1, GATE_U, 2)
+            on(add_turned, j - 1, GATE_U, (0,))
+            on(add_turned, j - 1, GATE_U, (1,))
+            on(add_turned, j - 1, GATE_U, (2,))
+            on(add_turned, j - 1, GATE_U, (3,))
+            on(state_pass, j - 1, GATE_U, 3)
+            on(update_gate, j - 1, None)
+            on(attention_gate, j - 1)
+            on(step_finish, j - 2, None)
             on(quantize, j + 1, "x")
-            if j == 0:
-                make_g_diag()
             on(gained_state, j)
+            on(reset_state, j)
+            on(candidate_proj, j - 1)
+            on(candidate, j - 1)
             on(state_pass, j + 1, GATE_R, 0)
             on(turn_h, j + 2)
             on(copy_hT, j + 2)
+            on(step_delta, j - 1)
+            on(widen_x, j + 3)
             on(state_pass, j + 1, GATE_R, 1)
             on(state_pass, j + 1, GATE_R, 2)
             on(state_pass, j + 1, GATE_R, 3)
             on(copy_state_proj, j + 1, GATE_R)
 
         last = TILES - 1
-        on(x_proj, last, GATE_U)
+        on(x_proj_turned, last - 1, GATE_U)
+        on(x_proj, last, GATE_R)
+        on(copy_proj, last - 1, GATE_U)
+        on(add_proj, last, GATE_R)
+        on(x_proj, last - 1, GATE_A)
+        on(gained_state, last)
+        on(turn_s, last - 1)
+        on(gather_words, last - 1, "s")
+        on(gate_sigmoid, last, GATE_R)
+        on(step_scale, last - 2, None)
+        on(quantize, last - 1, "s")
+        on(attention_dot, last - 1)
+        on(state_pass, last - 1, GATE_U, 0)
+        on(state_pass, last - 1, GATE_U, 1)
+        on(state_pass, last - 1, GATE_U, 2)
+        on(add_turned, last - 1, GATE_U, (0,))
+        on(add_turned, last - 1, GATE_U, (1,))
+        on(add_turned, last - 1, GATE_U, (2,))
+        on(add_turned, last - 1, GATE_U, (3,))
+        on(state_pass, last - 1, GATE_U, 3)
+        on(candidate_proj, last - 1)
+        on(x_proj_turned, last, GATE_U)
         on(x_proj, last, GATE_A)
         on(reset_state, last)
+        on(attention_gate, last - 1)
+        on(candidate, last - 1)
+        on(step_finish, last - 2, None)
+        on(state_pass, last, GATE_U, 0)
         on(turn_s, last)
         on(gather_words, last, "s")
-        on(add_proj, last, GATE_U)
-        on(gate_sigmoid, last, GATE_U)
-        on(step_scale, last - 2)
-        on(candidate_proj, last - 1)
-        on(candidate, last - 1)
-        on(quantize, last, "s")
-        on(candidate_proj, last)
-        on(attention_dot, last)
-        on(attention_gate, last)
-        on(candidate, last)
-        on(step_finish, last - 2)
+        on(update_gate, last - 1, None)
         on(step_delta, last - 1)
+        on(quantize, last, "s")
+        on(state_pass, last, GATE_U, 1)
+        on(candidate_proj, last)
+        on(copy_proj, last, GATE_U)
+        on(candidate, last)
+        on(attention_dot, last)
+        on(step_scale, last - 1, None)
+        on(attention_gate, last)
+        on(state_pass, last, GATE_U, 2)
+        on(add_turned, last, GATE_U, (0,))
+        on(add_turned, last, GATE_U, (1,))
+        on(add_turned, last, GATE_U, (2,))
+        on(add_turned, last, GATE_U, (3,))
+        on(state_pass, last, GATE_U, 3)
         on(step_delta, last)
-        on(step_scale, last - 1)
-        on(step_scale, last)
-        on(step_finish, last - 1)
-        on(step_finish, last)
+        on(update_gate, last, 0)
+        on(update_gate, last, 1)
+        on(step_finish, last - 1, None)
+        on(step_scale, last, 0)
+        on(step_scale, last, 1)
+        on(step_finish, last, 0)
+        on(step_finish, last, 1)

@@ -77,23 +77,24 @@ def tile_dienaugrustep_w8_kernel(
         warm = keep.tile([P, 1], F32, name="warm")
         nc.scalar.activation(out=warm[:], in_=ident[:, 0:1], func=ACT.Sigmoid)
 
+        xs4 = keep.tile([P, 4], F32, name="xs4")
+        nc.sync.dma_start(out=xs4[:], in_=x_scale.rearrange("o (p t) -> p (o t)", t=4))
+        load_rows(hs, "h_0", h_rows, 0, 1, BF16)
+        load_rows(xb, "xbytes_0", x_rows, 0, 1, U8)
+        load_uh("uh_0", 0)
+        load_rows(hs, "h_1", h_rows, 1, 1, BF16)
+        load_rows(xb, "xbytes_1", x_rows, 1, 3, U8)
+        g4 = keep.tile([P, 2, 2], BF16, name="g4")
+        nc.sync.dma_start(out=g4[:], in_=g.rearrange("(u p e) -> p u e", u=2, e=2))
+        load_uh("uh_1", 1)
         for q in range(4):
-            nc.gpsimd.dma_start(
+            nc.sync.dma_start(
                 out=wx_sc[32 * q : 32 * q + 16, :].bitcast(I32),
                 in_=wx_scales[0][4 * q : 4 * q + 4, :].bitcast(I32).rearrange("r (j n) -> j r n", j=4),
             )
-        xs4 = keep.tile([P, 4], F32, name="xs4")
-        nc.sync.dma_start(out=xs4[:], in_=x_scale.rearrange("o (p t) -> p (o t)", t=4))
-        load_rows(xb, "xbytes_0", x_rows, 0, 2, U8)
-        load_rows(hs, "h_0", h_rows, 0, 2, BF16)
-        g4 = keep.tile([P, 2, 2], BF16, name="g4")
-        nc.sync.dma_start(out=g4[:], in_=g.rearrange("(u p e) -> p u e", u=2, e=2))
-        load_uh("uh_0", 0)
-        load_uh("uh_1", 1)
         load_wx("wx_ur", GATE_U, 2)
         load_wx("wx_a", GATE_A, 1)
         load_rows(hs, "h_2", h_rows, 2, 2, BF16)
-        load_rows(xb, "xbytes_2", x_rows, 2, 2, U8)
         load_rows(ts, "t_0", t_rows, 0, 2, BF16)
         load_wx("wx_n", GATE_N, 1)
         un = keep.tile([P, D], U32, name="un", align_bytes=64)
@@ -114,6 +115,12 @@ def tile_dienaugrustep_w8_kernel(
 
         def wx_scale(gate):
             return wx_sc[4 * gate : P, :]
+
+        zeros = keep.tile([P, D], BF16, name="zeros")
+        nc.vector.memset(zeros[:], 0.0)
+        idle = bank()
+        for k in range(3):
+            nc.tensor.matmul(idle[:], lhsT=zeros[:, 0:P], rhs=zeros[:], start=True, stop=True)
 
         spread = bank()
         for k in range(4):

@@ -39,6 +39,8 @@ def tile_dienaugrustep_w8_kernel(
         ident = keep.tile([P, P], F32, name="ident")
         make_identity(nc, ident[:])
 
+        zeros = keep.tile([P, D], BF16, name="zeros")
+        nc.vector.memset(zeros[:], 0.0)
         wx_sc = keep.tile([P, D], U8, name="wx_sc", align_bytes=64)
         un_sc = keep.tile([P, D], U8, name="un_sc", align_bytes=64)
         nc.vector.memset(wx_sc[:].bitcast(I32), 0)
@@ -67,12 +69,12 @@ def tile_dienaugrustep_w8_kernel(
             for i in range(count):
                 wx[first + i] = dst[:, i * D : (i + 1) * D]
 
-        def load_uh(name, u):
-            dst = keep.tile([P, 2, 2 * D], BF16, name=name, align_bytes=64)
-            nc.sync.dma_start(out=dst[:], in_=uh_rows[u])
+        def load_uh(name, gate, u):
+            dst = keep.tile([P, 2, D], BF16, name=name, align_bytes=64)
+            first = (gate - GATE_U) * D
+            nc.sync.dma_start(out=dst[:], in_=uh_rows[u][:, :, first : first + D])
             for e in range(2):
-                uw[GATE_U, u, e] = dst[:, e, 0:D]
-                uw[GATE_R, u, e] = dst[:, e, D : 2 * D]
+                uw[gate, u, e] = dst[:, e, :]
 
         warm = keep.tile([P, 1], F32, name="warm")
         nc.scalar.activation(out=warm[:], in_=ident[:, 0:1], func=ACT.Sigmoid)
@@ -81,20 +83,23 @@ def tile_dienaugrustep_w8_kernel(
         nc.sync.dma_start(out=xs4[:], in_=x_scale.rearrange("o (p t) -> p (o t)", t=4))
         load_rows(hs, "h_0", h_rows, 0, 1, BF16)
         load_rows(xb, "xbytes_0", x_rows, 0, 1, U8)
-        load_uh("uh_0", 0)
-        load_rows(hs, "h_1", h_rows, 1, 1, BF16)
-        load_rows(xb, "xbytes_1", x_rows, 1, 3, U8)
         g4 = keep.tile([P, 2, 2], BF16, name="g4")
         nc.sync.dma_start(out=g4[:], in_=g.rearrange("(u p e) -> p u e", u=2, e=2))
-        load_uh("uh_1", 1)
+        load_uh("uh_r0", GATE_R, 0)
+        load_uh("uh_r1", GATE_R, 1)
+        load_rows(hs, "h_1", h_rows, 1, 1, BF16)
+        load_rows(xb, "xbytes_1", x_rows, 1, 3, U8)
+        load_wx("wx_r", GATE_R, 1)
         for q in range(4):
             nc.sync.dma_start(
                 out=wx_sc[32 * q : 32 * q + 16, :].bitcast(I32),
                 in_=wx_scales[0][4 * q : 4 * q + 4, :].bitcast(I32).rearrange("r (j n) -> j r n", j=4),
             )
-        load_wx("wx_ur", GATE_U, 2)
-        load_wx("wx_a", GATE_A, 1)
+        load_wx("wx_u", GATE_U, 1)
+        load_uh("uh_u0", GATE_U, 0)
+        load_uh("uh_u1", GATE_U, 1)
         load_rows(hs, "h_2", h_rows, 2, 2, BF16)
+        load_wx("wx_a", GATE_A, 1)
         load_rows(ts, "t_0", t_rows, 0, 2, BF16)
         load_wx("wx_n", GATE_N, 1)
         un = keep.tile([P, D], U32, name="un", align_bytes=64)
@@ -116,8 +121,6 @@ def tile_dienaugrustep_w8_kernel(
         def wx_scale(gate):
             return wx_sc[4 * gate : P, :]
 
-        zeros = keep.tile([P, D], BF16, name="zeros")
-        nc.vector.memset(zeros[:], 0.0)
         idle = bank()
         for k in range(3):
             nc.tensor.matmul(idle[:], lhsT=zeros[:, 0:P], rhs=zeros[:], start=True, stop=True)
@@ -358,12 +361,10 @@ def tile_dienaugrustep_w8_kernel(
             nc.sync.dma_start(out=out_rows[:, j, cols], in_=st["o", j][:, cols])
 
         def make_g_diag():
-            nc.vector.tensor_tensor(
-                out=g_diag[:],
-                in0=ident[:].unsqueeze(1).to_broadcast([P, 4, P]),
-                in1=g4[:].rearrange("p u e -> p (u e)").unsqueeze(2).to_broadcast([P, 4, P]),
-                op=ALU.mult,
-            )
+            g32 = keep.tile([P, 4], F32, name="g32")
+            nc.scalar.copy(out=g32[:], in_=g4[:].rearrange("p u e -> p (u e)"))
+            for k in range(4):
+                nc.scalar.activation(out=g_diag[:, k, :], in_=ident[:], func=ACT.Copy, scale=g32[:, k : k + 1])
 
         def on(fn, j, *args):
             if 0 <= j < TILES:
@@ -372,45 +373,45 @@ def tile_dienaugrustep_w8_kernel(
         on(widen_x, 0)
         on(turn_h, 0)
         on(copy_hT, 0)
-        on(turn_h, 1)
-        on(copy_hT, 1)
-        on(widen_x, 1)
         make_g_diag()
         on(state_pass, 0, GATE_R, 0)
         on(state_pass, 0, GATE_R, 1)
+        on(state_pass, 0, GATE_R, 2)
+        on(turn_h, 1)
+        on(copy_hT, 1)
+        on(state_pass, 0, GATE_R, 3)
         on(turn_x, 0)
         on(gather_words, 0, "x")
+        on(copy_state_proj, 0, GATE_R)
+        on(widen_x, 1)
         on(quantize, 0, "x")
         on(state_pass, 1, GATE_R, 0)
         on(state_pass, 1, GATE_R, 1)
-        on(state_pass, 0, GATE_R, 2)
-        on(state_pass, 0, GATE_R, 3)
-        on(copy_state_proj, 0, GATE_R)
+        on(widen_x, 2)
         on(turn_x, 1)
-        on(gather_words, 1, "x")
         on(state_pass, 1, GATE_R, 2)
         on(state_pass, 1, GATE_R, 3)
-        on(copy_state_proj, 1, GATE_R)
         on(x_proj, 0, GATE_R)
+        on(gather_words, 1, "x")
         on(add_proj, 0, GATE_R)
-        on(quantize, 1, "x")
+        on(copy_state_proj, 1, GATE_R)
         on(x_proj_turned, 0, GATE_U)
+        on(quantize, 1, "x")
         on(copy_proj, 0, GATE_U)
         on(gate_sigmoid, 0, GATE_R)
-        on(widen_x, 2)
         on(widen_x, 3)
         on(gained_state, 0)
         on(state_pass, 0, GATE_U, 0)
-        on(turn_h, 2)
-        on(copy_hT, 2)
         on(state_pass, 0, GATE_U, 1)
         on(state_pass, 0, GATE_U, 2)
+        on(reset_state, 0)
         on(add_turned, 0, GATE_U, (0,))
         on(add_turned, 0, GATE_U, (1,))
         on(add_turned, 0, GATE_U, (2,))
         on(add_turned, 0, GATE_U, (3,))
+        on(turn_h, 2)
+        on(copy_hT, 2)
         on(state_pass, 0, GATE_U, 3)
-        on(reset_state, 0)
         on(update_gate, 0, None)
 
         on(x_proj, 1, GATE_R)
@@ -430,8 +431,8 @@ def tile_dienaugrustep_w8_kernel(
         on(turn_h, 3)
         on(copy_hT, 3)
         on(state_pass, 2, GATE_R, 3)
-        on(widen_x, 4)
         on(quantize, 2, "x")
+        on(widen_x, 4)
         on(copy_state_proj, 2, GATE_R)
         on(gained_state, 1)
         on(reset_state, 1)
@@ -449,8 +450,8 @@ def tile_dienaugrustep_w8_kernel(
             on(turn_s, j - 1)
             on(gather_words, j - 1, "s")
             on(gate_sigmoid, j, GATE_R)
-            on(step_scale, j - 2, None)
             on(quantize, j - 1, "s")
+            on(step_scale, j - 2, None)
             on(state_pass, j - 1, GATE_U, 1)
             on(turn_x, j + 1)
             on(gather_words, j + 1, "x")
@@ -504,13 +505,13 @@ def tile_dienaugrustep_w8_kernel(
         on(x_proj_turned, last, GATE_U)
         on(x_proj, last, GATE_A)
         on(reset_state, last)
-        on(attention_gate, last - 1)
+        on(update_gate, last - 1, None)
         on(candidate, last - 1)
+        on(attention_gate, last - 1)
         on(step_finish, last - 2, None)
         on(state_pass, last, GATE_U, 0)
         on(turn_s, last)
         on(gather_words, last, "s")
-        on(update_gate, last - 1, None)
         on(step_delta, last - 1)
         on(quantize, last, "s")
         on(state_pass, last, GATE_U, 1)

import math
from contextlib import ExitStack

import concourse.mybir as mybir
from concourse.masks import make_identity

B, D = 1024, 512
FLOPS = 2 * B * D * (4 * D + 2 * D + D)

F32 = mybir.dt.float32
BF16 = mybir.dt.bfloat16
I32 = mybir.dt.int32
U32 = mybir.dt.uint32
U8 = mybir.dt.uint8
FP8 = mybir.dt.float8_e4m3fn
FP8X4 = mybir.dt.float8_e4m3fn_x4
ACT = mybir.ActivationFunctionType
ALU = mybir.AluOpType

P = 128
TILES = B // P
GP_TILES = 0
GATE_A, GATE_U, GATE_R, GATE_N = 0, 1, 2, 3


def tile_dienaugrustep_w8_kernel(
    tc, x_bytes, x_scale, h, t, wx_words, wx_scales, uh, g, un_words, un_scales, out
):
    nc = tc.nc
    with ExitStack() as ctx:
        keep = ctx.enter_context(tc.tile_pool(name="keep", bufs=1))
        work = ctx.enter_context(tc.tile_pool(name="work", bufs=4))
        psum = ctx.enter_context(tc.psum_pool(name="psum", bufs=8))
        ctx.enter_context(tc.manual_schedule())

        def bank():
            return psum.tile([P, D], F32, name="bank", tag="bank")

        ident = keep.tile([P, P], F32, name="ident")
        make_identity(nc, ident[:])

        zeros = keep.tile([P, D], BF16, name="zeros")
        nc.vector.memset(zeros[:], 0.0)
        wx_sc = keep.tile([P, D], U8, name="wx_sc", align_bytes=64)
        un_sc = keep.tile([P, D], U8, name="un_sc", align_bytes=64)
        nc.vector.memset(wx_sc[:].bitcast(I32), 0)
        nc.vector.memset(un_sc[:].bitcast(I32), 0)

        x_rows = x_bytes.rearrange("(p i) k -> p i k", i=TILES)
        h_rows = h.rearrange("(p i) k -> p i k", i=TILES)
        t_rows = t.rearrange("(p i) k -> p i k", i=TILES)
        out_rows = out.rearrange("(p i) k -> p i k", i=TILES)
        wx_flat = wx_words[0].rearrange("p n t -> p (n t)")
        uh_rows = uh.rearrange("(u p e) n -> u p e n", u=2, e=2)

        xb, hs, ts, wx, uw = {}, {}, {}, {}, {}

        def load_rows(table, name, rows, first, count, dtype):
            dst = keep.tile([P, count, D], dtype, name=name, align_bytes=64)
            nc.sync.dma_start(out=dst[:], in_=rows[:, first : first + count, :])
            for i in range(count):
                table[first + i] = dst[:, i, :]

        def load_wx(name, first, count):
            dst = keep.tile([P, count * D], U32, name=name, align_bytes=64)
            nc.sync.dma_start(
                out=dst[:].bitcast(I32), in_=wx_flat[:, 4 * D * first : 4 * D * (first + count)].bitcast(I32)
            )
            for i in range(count):
                wx[first + i] = dst[:, i * D : (i + 1) * D]

        def load_uh(name, gate, u):
            dst = keep.tile([P, 2, D], BF16, name=name, align_bytes=64)
            first = (gate - GATE_U) * D
            nc.sync.dma_start(out=dst[:], in_=uh_rows[u][:, :, first : first + D])
            for e in range(2):
                uw[gate, u, e] = dst[:, e, :]

        warm = keep.tile([P, 1], F32, name="warm")
        nc.scalar.activation(out=warm[:], in_=ident[:, 0:1], func=ACT.Sigmoid)

        xs4 = keep.tile([P, 4], F32, name="xs4")
        nc.sync.dma_start(out=xs4[:], in_=x_scale.rearrange("o (p t) -> p (o t)", t=4))
        load_rows(hs, "h_0", h_rows, 0, 1, BF16)
        load_rows(xb, "xbytes_0", x_rows, 0, 1, U8)
        g4 = keep.tile([P, 2, 2], BF16, name="g4")
        nc.sync.dma_start(out=g4[:], in_=g.rearrange("(u p e) -> p u e", u=2, e=2))
        load_uh("uh_r0", GATE_R, 0)
        load_uh("uh_r1", GATE_R, 1)
        load_rows(hs, "h_1", h_rows, 1, 1, BF16)
        load_rows(xb, "xbytes_1", x_rows, 1, 3, U8)
        load_wx("wx_r", GATE_R, 1)
        for q in range(4):
            nc.sync.dma_start(
                out=wx_sc[32 * q : 32 * q + 16, :].bitcast(I32),
                in_=wx_scales[0][4 * q : 4 * q + 4, :].bitcast(I32).rearrange("r (j n) -> j r n", j=4),
            )
        load_wx("wx_u", GATE_U, 1)
        load_uh("uh_u0", GATE_U, 0)
        load_uh("uh_u1", GATE_U, 1)
        load_rows(hs, "h_2", h_rows, 2, 2, BF16)
        load_wx("wx_a", GATE_A, 1)
        load_rows(ts, "t_0", t_rows, 0, 2, BF16)
        load_wx("wx_n", GATE_N, 1)
        un = keep.tile([P, D], U32, name="un", align_bytes=64)
        nc.sync.dma_start(
            out=un[:].bitcast(I32), in_=un_words[0].rearrange("p n t -> p (n t)").bitcast(I32)
        )
        for q in range(4):
            nc.sync.dma_start(
                out=un_sc[32 * q : 32 * q + 4, :].bitcast(I32),
                in_=un_scales[0][4 * q : 4 * q + 4, :].bitcast(I32),
            )
        load_rows(xb, "xbytes_4", x_rows, 4, 4, U8)
        load_rows(hs, "h_4", h_rows, 4, 2, BF16)
        load_rows(ts, "t_2", t_rows, 2, 2, BF16)
        load_rows(hs, "h_6", h_rows, 6, 2, BF16)
        load_rows(ts, "t_4", t_rows, 4, 2, BF16)
        load_rows(ts, "t_6", t_rows, 6, 2, BF16)

        def wx_scale(gate):
            return wx_sc[4 * gate : P, :]

        idle = bank()
        for k in range(3):
            nc.tensor.matmul(idle[:], lhsT=zeros[:, 0:P], rhs=zeros[:], start=True, stop=True)

        spread = bank()
        for k in range(4):
            nc.tensor.transpose(
                spread[:, k * P : (k + 1) * P], xs4[:, k : k + 1].to_broadcast([P, P]), ident[:]
            )
        xs_all = keep.tile([P, D], F32, name="xs_all")
        nc.vector.tensor_copy(
            out=xs_all[:].rearrange("q (p t) -> q p t", t=4),
            in_=spread[:].rearrange("q (t p) -> q p t", t=4),
        )
        g_diag = keep.tile([P, 4, P], BF16, name="g_diag")

        st = {}

        def columns(part):
            if part is None:
                return slice(0, D)
            return slice(part * D // 2, (part + 1) * D // 2)

        def widen_x(j):
            xw = work.tile([P, D], BF16, name="xw", align_bytes=64)
            nc.vector.tensor_tensor(out=xw[:], in0=xb[j].bitcast(FP8), in1=xs_all[:], op=ALU.mult)
            st["xw", j] = xw

        def turn(key, j, words):
            b = bank()
            for u in range(2):
                nc.tensor.transpose(b[:, u * P : (u + 1) * P], words(u), ident[:])
            st[key, j] = b

        def turn_x(j):
            w = st["xw", j][:].bitcast(F32)
            turn("xT", j, lambda u: w[:, u : 2 * P : 2])

        def turn_h(j):
            w = hs[j].bitcast(F32)
            turn("hT", j, lambda u: w[:, u * P : (u + 1) * P])

        def turn_s(j):
            w = st["s", j][:].bitcast(F32)
            turn("sT", j, lambda u: w[:, u * P : (u + 1) * P])

        def gather_words(j, key):
            grouped = work.tile([P, D], BF16, name=key + "_grouped", align_bytes=64)
            nc.scalar.copy(
                out=grouped[:].bitcast(F32).rearrange("p (r u) -> p r u", u=2),
                in_=st[key + "T", j][:, 0 : 2 * P].rearrange("p (u r) -> p r u", u=2),
            )
            st[key + "g", j] = grouped

        def quantize(j, key):
            codes = work.tile([P, P], U32, name=key + "_codes", align_bytes=64)
            scales = work.tile([P, P], U8, name=key + "_scales", align_bytes=64)
            nc.vector.quantize_mx(out=codes[:].bitcast(FP8X4), scales=scales[:], in_=st[key + "g", j][:])
            st[key + "q", j] = (codes, scales)

        def copy_hT(j):
            hT = work.tile([P, 2 * P], F32, name="hT_words")
            nc.scalar.copy(out=hT[:], in_=st["hT", j][:, 0 : 2 * P])
            st["hTs", j] = hT

        def h_plane(j, u, e):
            return st["hTs", j][:].bitcast(BF16)[:, u * 2 * P + e : (u + 1) * 2 * P : 2]

        def mx_pass(b, operand, words, scale, start, stop):
            codes, scales = operand
            nc.tensor.matmul_mx(
                out=b[:],
                lhsT=codes[:].bitcast(FP8X4),
                lhsT_scale=scales[:],
                rhs=words.bitcast(FP8X4),
                rhs_scale=scale,
                start=start,
                stop=stop,
            )

        def x_proj(j, gate):
            b = bank()
            mx_pass(b, st["xq", j], wx[gate], wx_scale(gate), True, True)
            st["xp", gate, j] = b

        def x_proj_turned(j, gate):
            codes, scales = st["xq", j]
            b = bank()
            for c in range(4):
                cols = slice(c * P, (c + 1) * P)
                nc.tensor.matmul_mx(
                    out=b[:, cols],
                    lhsT=wx[gate][:, cols].bitcast(FP8X4),
                    lhsT_scale=wx_scale(gate)[:, cols],
                    rhs=codes[:].bitcast(FP8X4),
                    rhs_scale=scales[:],
                    start=True,
                    stop=True,
                )
            st["xp", gate, j] = b

        def copy_proj(j, gate):
            sb = work.tile([P, D], F32, name="xp_%d" % gate)
            nc.scalar.copy(out=sb[:], in_=st["xp", gate, j][:])
            st["xps", gate, j] = sb

        def add_turned(j, gate, blocks):
            for c in blocks:
                cols = slice(c * P, (c + 1) * P)
                nc.tensor.matmul(
                    st["z", gate, j][:, cols],
                    lhsT=st["xps", gate, j][:, cols],
                    rhs=ident[:],
                    start=False,
                    stop=False,
                    is_transpose=True,
                )

        def update_gate(j, part):
            if part != 1:
                st["gate", GATE_U, j] = work.tile([P, D], F32, name="gate_u")
            cols = columns(part)
            nc.scalar.activation(
                out=st["gate", GATE_U, j][:, cols], in_=st["z", GATE_U, j][:, cols], func=ACT.Sigmoid
            )

        def candidate_proj(j):
            b = bank()
            mx_pass(b, st["xq", j], wx[GATE_N], wx_scale(GATE_N), True, False)
            mx_pass(b, st["sq", j], un[:], un_sc[:], False, True)
            st["zn", j] = b

        def state_pass(j, gate, k):
            if k == 0:
                st["z", gate, j] = bank()
            nc.tensor.matmul(
                st["z", gate, j][:],
                lhsT=h_plane(j, k // 2, k % 2),
                rhs=uw[gate, k // 2, k % 2],
                start=(k == 0),
                stop=(k == 3),
            )

        def in_gate_order(gate, src):
            if gate == GATE_R:
                return src.rearrange("q (p u e) -> q u p e", u=2, e=2)
            return src

        def as_gate_shape(gate, dst):
            if gate == GATE_R:
                return dst.rearrange("q (u p e) -> q u p e", u=2, e=2)
            return dst

        def copy_state_proj(j, gate):
            sb = work.tile([P, D], F32, name="hp_%d" % gate)
            nc.scalar.copy(out=as_gate_shape(gate, sb[:]), in_=in_gate_order(gate, st["z", gate, j][:]))
            st["hp", gate, j] = sb

        def add_proj(j, gate):
            z = work.tile([P, D], F32, name="z_%d" % gate)
            nc.vector.tensor_tensor(
                out=as_gate_shape(gate, z[:]),
                in0=in_gate_order(gate, st["xp", gate, j][:]),
                in1=as_gate_shape(gate, st["hp", gate, j][:]),
                op=ALU.add,
            )
            st["zs", gate, j] = z

        def gate_sigmoid(j, gate):
            y = work.tile([P, D], F32, name="gate_%d" % gate)
            nc.scalar.activation(out=y[:], in_=st["zs", gate, j][:], func=ACT.Sigmoid)
            st["gate", gate, j] = y

        def gained_state(j):
            b = bank()
            for u in range(2):
                for e in range(2):
                    c = 2 * e + u
                    nc.tensor.matmul(
                        b[:, c * P : (c + 1) * P],
                        lhsT=h_plane(j, u, e),
                        rhs=g_diag[:, 2 * u + e, :],
                        start=True,
                        stop=True,
                    )
            st["hg", j] = b

        def attention_dot(j):
            prod = work.tile([P, D], F32, name="prod")
            dot = work.tile([P, 1], F32, name="dot")
            nc.vector.scalar_tensor_tensor(
                out=prod[:], in0=st["xp", GATE_A, j][:], scalar=1.0 / math.sqrt(D), in1=ts[j],
                op0=ALU.mult, op1=ALU.mult, accum_out=dot[:],
            )
            st["dot", j] = dot

        def attention_gate(j):
            a = work.tile([P, 1], F32, name="a")
            nc.scalar.activation(out=a[:], in_=st["dot", j][:], func=ACT.Sigmoid)
            st["a", j] = a

        def reset_state(j):
            s = work.tile([P, D], BF16, name="s", align_bytes=64)
            nc.vector.tensor_tensor(
                out=s[:].rearrange("q (u p e) -> q u p e", u=2, e=2),
                in0=st["hg", j][:].rearrange("q (e p u) -> q u p e", u=2, e=2),
                in1=st["gate", GATE_R, j][:].rearrange("q (u p e) -> q u p e", u=2, e=2),
                op=ALU.mult,
            )
            st["s", j] = s

        def candidate(j):
            n = work.tile([P, D], F32, name="n")
            nc.scalar.activation(out=n[:], in_=st["zn", j][:], func=ACT.Tanh)
            st["n", j] = n

        def step_delta(j):
            d = work.tile([P, D], F32, name="d")
            nc.vector.tensor_tensor(out=d[:], in0=st["n", j][:], in1=hs[j], op=ALU.subtract)
            st["d", j] = d

        def step_scale(j, part):
            if part != 1:
                st["m", j] = work.tile([P, D], F32, name="m")
            cols = columns(part)
            nc.vector.tensor_tensor(
                out=st["m", j][:, cols], in0=st["gate", GATE_U, j][:, cols], in1=st["d", j][:, cols], op=ALU.mult
            )

        def step_finish(j, part):
            if part != 1:
                st["o", j] = work.tile([P, D], F32, name="o")
            cols = columns(part)
            nc.vector.scalar_tensor_tensor(
                out=st["o", j][:, cols], in0=st["m", j][:, cols], scalar=st["a", j][:], in1=hs[j][:, cols],
                op0=ALU.mult, op1=ALU.add,
            )
            nc.sync.dma_start(out=out_rows[:, j, cols], in_=st["o", j][:, cols])

        def make_g_diag():
            g32 = keep.tile([P, 4], F32, name="g32")
            nc.scalar.copy(out=g32[:], in_=g4[:].rearrange("p u e -> p (u e)"))
            for k in range(4):
                nc.scalar.activation(out=g_diag[:, k, :], in_=ident[:], func=ACT.Copy, scale=g32[:, k : k + 1])

        def on(fn, j, *args):
            if 0 <= j < TILES:
                fn(j, *args)

        on(widen_x, 0)
        on(turn_h, 0)
        on(copy_hT, 0)
        make_g_diag()
        on(state_pass, 0, GATE_R, 0)
        on(state_pass, 0, GATE_R, 1)
        on(state_pass, 0, GATE_R, 2)
        on(turn_h, 1)
        on(copy_hT, 1)
        on(state_pass, 0, GATE_R, 3)
        on(turn_x, 0)
        on(gather_words, 0, "x")
        on(copy_state_proj, 0, GATE_R)
        on(widen_x, 1)
        on(quantize, 0, "x")
        on(state_pass, 1, GATE_R, 0)
        on(state_pass, 1, GATE_R, 1)
        on(widen_x, 2)
        on(turn_x, 1)
        on(state_pass, 1, GATE_R, 2)
        on(state_pass, 1, GATE_R, 3)
        on(x_proj, 0, GATE_R)
        on(gather_words, 1, "x")
        on(add_proj, 0, GATE_R)
        on(copy_state_proj, 1, GATE_R)
        on(x_proj_turned, 0, GATE_U)
        on(quantize, 1, "x")
        on(copy_proj, 0, GATE_U)
        on(gate_sigmoid, 0, GATE_R)
        on(widen_x, 3)
        on(gained_state, 0)
        on(state_pass, 0, GATE_U, 0)
        on(state_pass, 0, GATE_U, 1)
        on(state_pass, 0, GATE_U, 2)
        on(reset_state, 0)
        on(add_turned, 0, GATE_U, (0,))
        on(add_turned, 0, GATE_U, (1,))
        on(add_turned, 0, GATE_U, (2,))
        on(add_turned, 0, GATE_U, (3,))
        on(turn_h, 2)
        on(copy_hT, 2)
        on(state_pass, 0, GATE_U, 3)
        on(update_gate, 0, None)

        on(x_proj, 1, GATE_R)
        on(add_proj, 1, GATE_R)
        on(x_proj, 0, GATE_A)
        on(state_pass, 2, GATE_R, 0)
        on(turn_s, 0)
        on(gather_words, 0, "s")
        on(gate_sigmoid, 1, GATE_R)
        on(attention_dot, 0)
        on(quantize, 0, "s")
        on(state_pass, 2, GATE_R, 1)
        on(turn_x, 2)
        on(gather_words, 2, "x")
        on(attention_gate, 0)
        on(state_pass, 2, GATE_R, 2)
        on(turn_h, 3)
        on(copy_hT, 3)
        on(state_pass, 2, GATE_R, 3)
        on(quantize, 2, "x")
        on(widen_x, 4)
        on(copy_state_proj, 2, GATE_R)
        on(gained_state, 1)
        on(reset_state, 1)
        on(candidate_proj, 0)
        on(candidate, 0)
        on(step_delta, 0)

        for j in range(2, TILES - 1):
            on(x_proj_turned, j - 1, GATE_U)
            on(x_proj, j, GATE_R)
            on(copy_proj, j - 1, GATE_U)
            on(add_proj, j, GATE_R)
            on(x_proj, j - 1, GATE_A)
            on(state_pass, j - 1, GATE_U, 0)
            on(turn_s, j - 1)
            on(gather_words, j - 1, "s")
            on(gate_sigmoid, j, GATE_R)
            on(quantize, j - 1, "s")
            on(step_scale, j - 2, None)
            on(state_pass, j - 1, GATE_U, 1)
            on(turn_x, j + 1)
            on(gather_words, j + 1, "x")
            on(attention_dot, j - 1)
            on(state_pass, j - 1, GATE_U, 2)
            on(add_turned, j - 1, GATE_U, (0,))
            on(add_turned, j - 1, GATE_U, (1,))
            on(add_turned, j - 1, GATE_U, (2,))
            on(add_turned, j - 1, GATE_U, (3,))
            on(state_pass, j - 1, GATE_U, 3)
            on(update_gate, j - 1, None)
            on(attention_gate, j - 1)
            on(step_finish, j - 2, None)
            on(quantize, j + 1, "x")
            on(gained_state, j)
            on(reset_state, j)
            on(candidate_proj, j - 1)
            on(candidate, j - 1)
            on(state_pass, j + 1, GATE_R, 0)
            on(turn_h, j + 2)
            on(copy_hT, j + 2)
            on(step_delta, j - 1)
            on(widen_x, j + 3)
            on(state_pass, j + 1, GATE_R, 1)
            on(state_pass, j + 1, GATE_R, 2)
            on(state_pass, j + 1, GATE_R, 3)
            on(copy_state_proj, j + 1, GATE_R)

        last = TILES - 1
        on(x_proj_turned, last - 1, GATE_U)
        on(x_proj, last, GATE_R)
        on(copy_proj, last - 1, GATE_U)
        on(add_proj, last, GATE_R)
        on(x_proj, last - 1, GATE_A)
        on(gained_state, last)
        on(turn_s, last - 1)
        on(gather_words, last - 1, "s")
        on(gate_sigmoid, last, GATE_R)
        on(step_scale, last - 2, None)
        on(quantize, last - 1, "s")
        on(attention_dot, last - 1)
        on(state_pass, last - 1, GATE_U, 0)
        on(state_pass, last - 1, GATE_U, 1)
        on(state_pass, last - 1, GATE_U, 2)
        on(add_turned, last - 1, GATE_U, (0,))
        on(add_turned, last - 1, GATE_U, (1,))
        on(add_turned, last - 1, GATE_U, (2,))
        on(add_turned, last - 1, GATE_U, (3,))
        on(state_pass, last - 1, GATE_U, 3)
        on(candidate_proj, last - 1)
        on(x_proj_turned, last, GATE_U)
        on(x_proj, last, GATE_A)
        on(reset_state, last)
        on(update_gate, last - 1, None)
        on(candidate, last - 1)
        on(attention_gate, last - 1)
        on(step_finish, last - 2, None)
        on(state_pass, last, GATE_U, 0)
        on(turn_s, last)
        on(gather_words, last, "s")
        on(step_delta, last - 1)
        on(quantize, last, "s")
        on(state_pass, last, GATE_U, 1)
        on(candidate_proj, last)
        on(copy_proj, last, GATE_U)
        on(candidate, last)
        on(attention_dot, last)
        on(step_scale, last - 1, None)
        on(attention_gate, last)
        on(state_pass, last, GATE_U, 2)
        on(add_turned, last, GATE_U, (0,))
        on(add_turned, last, GATE_U, (1,))
        on(add_turned, last, GATE_U, (2,))
        on(add_turned, last, GATE_U, (3,))
        on(state_pass, last, GATE_U, 3)
        on(step_delta, last)
        on(update_gate, last, 0)
        on(update_gate, last, 1)
        on(step_finish, last - 1, None)
        on(step_scale, last, 0)
        on(step_scale, last, 1)
        on(step_finish, last, 0)
        on(step_finish, last, 1)
